import numpy as np
CORES = [34,162,290,418,42,426]
N = 6
V, DEP = 16384, 8
def entries(a): return a.T.reshape(-1)
def pack(v, P): return np.ascontiguousarray(np.asarray(v, np.int32).reshape(-1, P).T)
def forest(rng, n, lev):
    P = np.arange(n)
    for l in range(1, int(lev.max()) + 1):
        a, b = np.nonzero(lev == l)[0], np.nonzero(lev == l - 1)[0]; P[a] = b[rng.integers(0, len(b), len(a))]
    return P
def lists(rng, how):
    n = N * V; P = np.arange(n)
    if how == "uniform":
        lev = rng.integers(0, DEP + 1, n); lev[rng.permutation(n)[:DEP + 1]] = np.arange(DEP + 1); P = forest(rng, n, lev)
    if how == "star":
        lev = np.ones(n, np.int64); lev[rng.permutation(n)[:4]] = 0; P = forest(rng, n, lev)
    if how == "chain":
        W = np.stack([V * r + rng.permutation(V)[:V // (DEP + 1) * (DEP + 1)].reshape(-1, DEP + 1) for r in range(N)]); P[W[:, :, 1:]] = np.roll(W, 1, axis=0)[:, :, :-1]
    if how == "deep":
        z = rng.permutation(N); g = V * z[1 + np.arange(DEP) % (N - 1)] + rng.permutation(V)[:DEP]; P[:] = g[-1]; P[g] = np.concatenate([g[:1], g[:-1]])
    if how == "whole":
        o = rng.permutation(N)
        for i in range(1, N - 1):
            if i % (DEP + 1): P[V * o[i]:V * o[i] + V] = V * o[i - 1] + rng.permutation(V)
        P[V * o[-1]:V * o[-1] + V] = V * o[-1] + forest(rng, V, rng.permutation(np.concatenate([np.arange(DEP + 1), rng.integers(0, DEP + 1, V - DEP - 1)])))
    return {"par": np.stack([pack(p, 16) for p in P.reshape(N, V)])}
def setup_inputs(rng):
    return dict({"val": rng.standard_normal((N, 16, V // 16), dtype=np.float32)}, **lists(rng, "uniform"))
def setup_inputs_chain(rng):
    d = setup_inputs(rng); d.update(lists(rng, "chain"))
    for k in ("val",): d[k] = (d[k].astype(np.float32) * 1048576.0).astype(d[k].dtype)
    return d
def setup_inputs_deep(rng):
    d = setup_inputs(rng); d.update(lists(rng, "deep"))
    for k in ("val",): d[k] = (d[k].astype(np.float32) * (1 / 1024.0)).astype(d[k].dtype)
    return d
def setup_inputs_star(rng):
    d = setup_inputs(rng); d.update(lists(rng, "star"))
    return d
def setup_inputs_whole(rng):
    d = setup_inputs(rng); d.update(lists(rng, "whole"))
    return d
def check_inputs(x):
    bad = []
    if x["par"].min() < 0 or x["par"].max() >= N * V: bad.append("par out of range")
    p = np.concatenate([entries(a) for a in x["par"]]); q = p
    for k in range(DEP - 1): q = p[q]
    if (p[q] != q).any(): bad.append("a node is more than DEP hops from a root")
    return bad
def reference(val, par):
    p = np.concatenate([entries(a) for a in par]); v = np.concatenate([entries(a) for a in val])
    q = p
    for k in range(DEP - 1): q = p[q]
    return {"y": np.stack([np.ascontiguousarray(v[q][V * r:V * r + V].reshape(-1, 16).T) for r in range(N)])}

from concourse.bass import DstId, RemoteDMATransfer
from concourse.mybir import AluOpType as Op, ActivationFunctionType as Act

R = 6
HOPS = 7
SETS = 2
SCRATCH = {
    "ptile": ("sbuf", [128, 128], "int32"),
    "e1": ("sbuf", [128, 128], "int32"),
    "e2": ("sbuf", [128, 128], "int32"),
    "e3": ("sbuf", [128, 128], "float32"),
    "enc": ("sbuf", [128, 128], "float32"),
    "win": ("sbuf", [128, 1024 * R], "float32"),
    "vwin": ("sbuf", [128, 1024 * R], "float32"),
    "q0": ("sbuf", [128, 16], "float32"),
    "hi0": ("sbuf", [128, 16], "bfloat16"),
    "hf0": ("sbuf", [128, 16], "float32"),
    "lo0": ("sbuf", [128, 16], "float32"),
    "ioG": ("sbuf", [128, 128], "int32"),
    "ioU": ("sbuf", [128, 128], "int32"),
    "ioE": ("sbuf", [128, 8], "int32"),
    "ioC": ("sbuf", [128, 1], "int32"),
    "shG": ("sbuf", [128, 128], "int32"),
    "shU": ("sbuf", [128, 128], "int32"),
    "shE": ("sbuf", [128, 8], "int32"),
    "shC": ("sbuf", [128, 1], "int32"),
    "G": ("sbuf", [128, 128], "bfloat16"),
    "Uf": ("sbuf", [128, 128], "float32"),
    "Ef": ("sbuf", [128, 8], "float32"),
    "En": ("sbuf", [128, 8], "bfloat16"),
    "ctr": ("sbuf", [128, 1], "float32"),
    "mine": ("sbuf", [128, 16], "float32"),
    "coll": ("sbuf", [128, 128], "float32"),
    "mk": ("psum", [128, 512], "float32"),
    "vown": ("dram", [8, 128, 16], "float32"),
}
for _s in range(SETS):
    SCRATCH.update({
        "ga_%d" % _s: ("sbuf", [128, 128], "float32"),
        "mh_%d" % _s: ("sbuf", [128, 128], "bfloat16"),
        "mf_%d" % _s: ("sbuf", [128, 128], "float32"),
        "ex_%d" % _s: ("sbuf", [128, 128], "bfloat16"),
        "off%d" % _s: ("sbuf", [128, 8], "uint16"),
        "bc_%d" % _s: ("psum", [128, 512], "float32"),
        "z_%d" % _s: ("psum", [128, 512], "float32"),
        "r_%d" % _s: ("psum", [128, 512], "float32"),
    })
for _r in range(R):
    SCRATCH["par%d" % _r] = ("dram", [128, 128], "float32")
    SCRATCH["val%d" % _r] = ("dram", [128, 128], "float32")

SEMAPHORES = (["ldp", "st", "sv", "sw", "e", "io_s", "c", "q0s", "wx", "wv", "i0", "res", "fin", "ys", "sent", "ow"]
              + ["%s%d" % (n, s) for n in ("ga", "mh", "mf", "r", "z", "ex", "bc", "lt", "of") for s in range(SETS)]
              + ["ap%d" % r for r in range(R)] + ["av%d" % r for r in range(R)])


def _chip_of(core, topo):
    return [c for c in range(512) if topo.host(c) == topo.host(core) and topo.chip(c) == topo.chip(core)]


def _roles(core, T, topo):
    same_rack = lambda a, b: topo.rack(topo.host(a)) == topo.rack(topo.host(b))
    mates_of = lambda a: [b for b in T.cores if b != a and same_rack(a, b)]
    partner = [b for b in T.cores if not same_rack(core, b) and topo.chip(b) == topo.chip(core) and topo.may_write(core, b)][0]
    sib = [c for c in _chip_of(core, topo) if c != core]
    near = [c for c in sib if topo.die(c) == topo.die(core)]
    far = [c for c in sib if topo.die(c) != topo.die(core)]
    rm, relayed = mates_of(core), mates_of(partner)
    entry = {"par": {core: core, partner: near[2], rm[0]: near[0], relayed[0]: near[1], rm[1]: far[0], relayed[1]: far[1]},
             "val": {core: core, partner: far[3], rm[0]: near[0], relayed[0]: near[1], rm[1]: far[2], relayed[1]: far[1]}}
    return rm, partner, relayed, entry


def _split(mask, n):
    bits = [b for b in range(16) if (mask >> b) & 1]
    m = len(bits) // n
    return [sum(1 << b for b in bits[m * i:m * i + m]) for i in range(n)]


def rank_program(g, core, T, topo):
    home = [c for c in T.cores if topo.host(c) == topo.host(core) and topo.chip(c) == topo.chip(core)]
    if not home:
        return
    home = home[0]
    chip = _chip_of(core, topo)
    k = chip.index(core)
    sibs = [c for c in chip if c != core]
    rm, partner, relayed, entry = _roles(home, T, topo)
    own = T.rank_of(home)
    is_rank = core == home
    last = [c for c in chip if c != home][-1]
    vec, ten, sca, syn = g.vector, g.tensor, g.scalar, g.sync
    tot, mx = {}, {}

    def inc(ins, sem, n=1):
        ins.then_inc(T.sem[sem], n)
        tot[sem] = tot.get(sem, 0) + n

    def wait(q, sem, val):
        q.wait_ge(T.sem[sem], val)
        mx[sem] = max(mx.get(sem, 0), val)

    def nbits(m):
        return sum((m >> b) & 1 for b in range(16))

    def fused(moves):
        trs = []
        for buf_in, buf_out, sem, dsts, mask in moves:
            ids = []
            for d in dsts:
                rid, pid = topo.addr(d, core)
                ids.append(DstId(rid=rid, pnc=pid))
            trs.append(RemoteDMATransfer(dst_ids=ids, dma_engine_mask=mask, remote_sem=T.sem[sem], srcs=[buf_in],
                                         dsts=[buf_out] * len(dsts)))
            tot["sent"] = tot.get("sent", 0) + nbits(mask)
        g.remote_dma_fused(trs, local_sem=T.sem["sent"])

    def send(buf_in, buf_out, sem, dsts, mask):
        fused([(buf_in, buf_out, sem, dsts, mask)])

    def arrive_count(kind, r):
        src_core = T.cores[r]
        ent = entry[kind][src_core]
        if ent != core:
            return nbits(topo.mask(ent, core))
        if src_core in relayed:
            return nbits(topo.mask(_roles(partner, T, topo)[3][kind][src_core], core))
        return nbits(topo.mask(src_core, core))

    order = [own] + [T.rank_of(c) for c in rm] + [T.rank_of(partner)] + [T.rank_of(c) for c in relayed]
    own_par, own_val = T["par%d" % own], T["val%d" % own]

    if is_rank:
        inc(syn.dma_start(T.ptile[:], T.par[:]), "ldp", 16)
        inc(sca.dma_start(T.vown[:], T.val[:]), "sv", 16)
        inc(sca.dma_start(own_val[:], T.val[:]), "sw", 16)

    inc(g.iota(T.ioG[:], [[-16, 8], [0, 16]], 0, 1), "io_s")
    inc(g.iota(T.ioU[:], [[-1, 128]], 128, 1), "io_s")
    inc(g.iota(T.ioE[:], [[-16, 8]], 0, 1), "io_s")
    inc(g.iota(T.ioC[:], [[0, 1]], 0, 1), "io_s")

    if is_rank:
        P = T.ptile[:]
        wait(vec, "ldp", 16)
        inc(vec.tensor_scalar(T.e1[:], P, 15, None, Op.bitwise_and), "e")
        inc(vec.tensor_scalar(T.e2[:], P, 4, None, Op.logical_shift_right), "e")
        wait(vec, "e", 2)
        inc(vec.tensor_scalar(T.e3[:], T.e1[:], 524288.0, 8388608.0, Op.mult, Op.add), "e")
        wait(vec, "e", 3)
        inc(vec.tensor_tensor(T.enc[:], T.e3[:], T.e2[:], Op.add), "e")
        wait(syn, "e", 4)
        inc(syn.dma_start(own_par[:], T.enc[:]), "st", 16)

    wait(vec, "io_s", 4)
    inc(vec.tensor_scalar(T.shG[:], T.ioG[:], 4, None, Op.arith_shift_right), "c")
    inc(vec.tensor_scalar(T.shU[:], T.ioU[:], 15, None, Op.bitwise_and), "c")
    inc(vec.tensor_scalar(T.shE[:], T.ioE[:], 4, None, Op.arith_shift_right), "c")
    inc(vec.tensor_scalar(T.shC[:], T.ioC[:], 15, None, Op.bitwise_and), "c")
    wait(vec, "c", 4)
    inc(vec.tensor_scalar(T.G[:], T.shG[:], 0, None, Op.is_equal), "c")
    inc(vec.tensor_scalar(T.Uf[:], T.shU[:], 0, None, Op.is_equal), "c")
    inc(vec.tensor_scalar(T.ctr[:], T.shC[:], 524288.0, 8388608.0, Op.mult, Op.add), "c")
    inc(vec.tensor_scalar(T.Ef[:], T.shE[:], 0, None, Op.is_equal), "c")
    inc(vec.tensor_scalar(T.En[:], T.shE[:], 0, -1.0, Op.is_equal, Op.mult), "c")
    NC = tot["c"]
    wait(vec, "c", NC)

    m16 = topo.mask(core, sibs[0])
    if is_rank:
        wait(g, "sv", 16)
        parts = _split(m16, 8)
        to = [(chip.index(c), c) for c in sibs] + [(k, last)]
        fused([(T.vown[i], T.vown[i], "ow", [c], parts[n]) for n, (i, c) in enumerate(to)])
        n_ow = 0
    else:
        n_ow = nbits(topo.mask(home, core)) // 8 * (2 if core == last else 1)
        wait(g, "ow", n_ow)
        rest = [c for c in sibs if c != home]
        pieces = [k] + ([chip.index(home)] if core == last else [])
        parts = _split(m16, len(pieces))
        fused([(T.vown[i], T.vown[i], "av%d" % own, rest, parts[n]) for n, i in enumerate(pieces)])
    n_own = sum(nbits(topo.mask(c, core)) for c in sibs if c != home)

    def pass_on(kind, sems):
        for r in order:
            src_core = T.cores[r]
            if entry[kind][src_core] != core:
                continue
            buf = T["%s%d" % (kind, r)][:]
            sem = "%s%d" % (sems, r)
            if is_rank:
                first = T.enc[:] if kind == "par" else buf
                wait(g, *(("e", 4) if kind == "par" else ("sw", 16)))
                dsts = [_roles(c, T, topo)[3][kind][core] for c in rm]
                send(first, buf, sem, dsts, topo.mask(core, dsts[0]))
                d = _roles(partner, T, topo)[3][kind][core]
                send(first, buf, sem, [d], topo.mask(core, d))
                if kind == "val":
                    continue
                wait(g, "st", 16)
            else:
                wait(g, sem, arrive_count(kind, r))
                if src_core in rm:
                    d = _roles(partner, T, topo)[3][kind][src_core]
                    send(buf, buf, sem, [d], topo.mask(core, d))
            send(buf, buf, sem, sibs, m16)

    pass_on("par", "ap")
    pass_on("val", "av")

    def ready(q, kind, r):
        if r == own and is_rank:
            wait(q, *(("st", 16) if kind == "par" else ("sw", 16)))
        elif r == own and kind == "val":
            wait(q, "ow", n_ow)
            wait(q, "av%d" % own, n_own)
        else:
            wait(q, ("ap%d" if kind == "par" else "av%d") % r, arrive_count(kind, r))

    for r in order:
        b = T["par%d" % r]
        ready(sca, "par", r)
        ready(syn, "par", r)
        if r == own:
            inc(sca.dma_start(T.q0[:], b[:, 16 * k:16 * k + 16]), "q0s", 16)
        for gr in range(8):
            q = sca if gr % 2 else syn
            inc(q.dma_start(T.win[16 * gr:16 * gr + 16, 1024 * r:1024 * r + 1024], b[:]), "wx", 16)
    for r in order:
        ready(syn, "val", r)
        src = T.vown[:] if r == own and not is_rank else T["val%d" % r][:]
        for gr in range(8):
            inc(syn.dma_start(T.vwin[16 * gr:16 * gr + 16, 1024 * r:1024 * r + 1024], src), "wv", 16)

    def mask(s, n):
        wait(vec, "bc%d" % s, n + 1)
        inc(vec.tensor_scalar(T.mk[:, 128 * s:128 * s + 128], T["bc_%d" % s][:, 0:128], T.ctr[:], None, Op.is_equal), "lt%d" % s)

    def offsets(s, h):
        wait(vec, "z%d" % s, h + 1)
        inc(vec.tensor_copy(T["off%d" % s][:], T["z_%d" % s][:, 0:8]), "of%d" % s)

    def expand(s, h):
        wait(vec, "r%d" % s, h + 1)
        inc(vec.tensor_tensor(T["ex_%d" % s][:], T["r_%d" % s][:, 0:128], T.Uf[:], Op.mult), "ex%d" % s)

    wait(vec, "q0s", 16)
    inc(vec.tensor_copy(T.hi0[:], T.q0[:]), "i0")
    wait(vec, "i0", 1)
    inc(vec.tensor_copy(T.hf0[:], T.hi0[:]), "i0")
    inc(vec.tensor_tensor(T.lo0[:], T.q0[:], T.hi0[:], Op.subtract), "i0")
    wait(vec, "i0", 3)
    for s in range(SETS):
        inc(vec.tensor_copy(T["off%d" % s][:], T.lo0[:, 8 * s:8 * s + 8]), "of%d" % s)
        for c in range(8):
            inc(vec.tensor_scalar(T["ex_%d" % s][:, 16 * c:16 * c + 16], T.Uf[:, 16 * c:16 * c + 16],
                                  T.hf0[:, 8 * s + c:8 * s + c + 1], None, Op.mult), "ex%d" % s)
    E0 = 8
    for s in range(SETS):
        mask(s, 0)
    for h in range(HOPS + 1):
        for s in range(SETS):
            t, ht = 1 - s, h - 1 + s
            mk = T.mk[:, 128 * s:128 * s + 128]
            wait(vec, "lt%d" % s, h + 1)
            wait(vec, "ga%d" % s, h + 1)
            if h < HOPS:
                inc(vec.tensor_tensor(T["mh_%d" % s][:], T["ga_%d" % s][:], mk, Op.mult), "mh%d" % s)
            else:
                inc(vec.tensor_tensor(T["mf_%d" % s][:], T["ga_%d" % s][:], mk, Op.mult), "mf%d" % s)
            if 0 <= ht < HOPS:
                offsets(t, ht)
            if h < HOPS:
                inc(vec.tensor_tensor(T["mf_%d" % s][:], T["ga_%d" % s][:], mk, Op.mult), "mf%d" % s)
            if 0 <= ht < HOPS:
                mask(t, ht + 1)
            if h < HOPS:
                expand(s, h)
    for s in range(SETS):
        wait(vec, "z%d" % s, HOPS + 1)
        res = T.coll[:, 16 * k + 8 * s:16 * k + 8 * s + 8] if is_rank else T.mine[:, 8 * s:8 * s + 8]
        inc(vec.tensor_copy(res, T["z_%d" % s][:, 0:8]), "res")

    wait(ten, "c", NC)

    def spread(s, n):
        wait(ten, "ex%d" % s, n + E0)
        inc(ten.matmul(T["bc_%d" % s][:, 0:128], T.G[:], T["ex_%d" % s][:], True, True), "bc%d" % s)

    for s in range(SETS):
        spread(s, 0)
    for h in range(HOPS):
        for s in range(SETS):
            wait(ten, "mh%d" % s, h + 1)
            inc(ten.matmul(T["r_%d" % s][:, 0:128], T["mh_%d" % s][:], T.G[:], True, True), "r%d" % s)
            wait(ten, "mf%d" % s, h + 1)
            ten.matmul(T["z_%d" % s][:, 0:8], T["mf_%d" % s][:], T.Ef[:], True, False)
            inc(ten.matmul(T["z_%d" % s][:, 0:8], T["mh_%d" % s][:], T.En[:], False, True), "z%d" % s)
            spread(s, h + 1)
    for s in range(SETS):
        wait(ten, "mf%d" % s, HOPS + 1)
        inc(ten.matmul(T["z_%d" % s][:, 0:8], T["mf_%d" % s][:], T.Ef[:], True, True), "z%d" % s)

    wait(sca, "wx", 16 * 8 * R)
    for h in range(HOPS + 1):
        if h == HOPS:
            wait(sca, "wv", 16 * 8 * R)
        for s in range(SETS):
            wait(sca, "of%d" % s, h + 1)
            w = T.win if h < HOPS else T.vwin
            inc(sca.activation(T["ga_%d" % s][:], w[:].indirect(T["off%d" % s][:]), Act.Copy), "ga%d" % s)

    if is_rank:
        n = sum(nbits(topo.mask(c, core)) for c in sibs)
        wait(syn, "res", SETS)
        wait(syn, "fin", n)
        inc(syn.dma_start(T.y[:], T.coll[:]), "ys", 16)
    else:
        wait(g, "res", SETS)
        send(T.mine[:], T.coll[:, 16 * k:16 * k + 16], "fin", [home], topo.mask(core, home))
    for sem in sorted(tot):
        if tot[sem] > mx.get(sem, 0):
            wait(g, sem, tot[sem])
